import numpy as np
import ml_dtypes


def mxq(x, axis, fmt="e4m3"):
    dtype, down = {"e4m3": (ml_dtypes.float8_e4m3fn, 7), "e5m2": (ml_dtypes.float8_e5m2, 14)}[fmt]
    v = np.moveaxis(np.asarray(x, np.float32).astype(ml_dtypes.bfloat16).astype(np.float64), axis, -1)
    blocks = v.reshape(v.shape[:-1] + (-1, 32))
    amax = np.abs(blocks).max(-1, keepdims=True)
    byte = np.maximum(np.where(amax > 0, np.frexp(amax)[1] - 1 + 127, 0) - down, 1)
    scale = np.exp2(byte - 127.0)
    codes = (blocks / scale).astype(np.float32).astype(dtype).astype(np.float64)
    return np.moveaxis((codes * scale).reshape(v.shape), -1, axis)


WIDE = False


def mx_kscale(k):
    if not WIDE:
        return np.ones(k)
    levels = np.array([30, -30])
    if k % 512:
        return np.exp2(np.random.permutation(np.resize(levels, k // 32))).repeat(32)
    a = np.empty((k // 512, 16))
    for p in range(k // 512):
        a[p, :8] = np.random.permutation(np.resize(levels, 8))
        for g in range(8):
            far = levels[np.abs(levels - a[p, g]) >= 10]
            a[p, g + 8] = far[np.random.randint(len(far))]
    return np.exp2(a.ravel()).repeat(32)


def f64(x):
    return np.asarray(x).astype(np.float64)


K, L, M, N = 1536, 1536, 256, 1024


def setup_inputs():
    n = np.random.standard_normal
    s1 = mx_kscale(K)[:, None]
    s2 = mx_kscale(L)[:, None]
    m1, m2 = np.exp(0.5 * n((1, M))), np.exp(0.5 * n((1, N)))
    return {
        "x": (n((K, M)) / np.sqrt(K) * s1).astype(np.float32),
        "xt": (n((K, N)) / s1).astype(np.float32),
        "g": (m1 * n((L, M)) / np.sqrt(L) * s2).astype(np.float32),
        "gt": (m2 * n((L, N)) / s2).astype(np.float32),
        "r": (n((256, 1024))).astype(np.float32),
    }


def reference(x, xt, g, gt, r):
    x_ = mxq(f64(x), 0, "e4m3")
    xt_ = mxq(f64(xt), 0, "e4m3")
    g_ = mxq(f64(g), 0, "e5m2")
    gt_ = mxq(f64(gt), 0, "e5m2")
    y = x_.T @ xt_
    u = g_.T @ gt_
    y = y * u
    return f64(r) + y

@@ -1,0 +1,174 @@
+from contextlib import ExitStack
+
+import concourse.mybir as mybir
+
+K, M, N = 1536, 256, 1024
+FLOPS = 2 * (2 * K * M * N)
+
+F32 = mybir.dt.float32
+BF16 = mybir.dt.bfloat16
+U32 = mybir.dt.uint32
+U8 = mybir.dt.uint8
+E4M3X4 = mybir.dt.float8_e4m3fn_x4
+E5M2X4 = mybir.dt.float8_e5m2_x4
+MULT = mybir.AluOpType.mult
+ADD = mybir.AluOpType.add
+
+P = 128
+PACK = 4
+K_PASS = P * PACK
+PASSES = K // K_PASS
+CAST_RUN = 4
+M_TILES = M // P
+HALF = N // 2
+
+STRIPS = ((0, HALF), (HALF, HALF // 2), (HALF + HALF // 2, HALF // 2))
+
+
+def tile_mix_ghost_res_kernel(tc, x, xt, g, gt, r, out):
+    nc = tc.nc
+    with ExitStack() as ctx:
+        raw = ctx.enter_context(tc.tile_pool(name="raw", bufs=1))
+        keep = ctx.enter_context(tc.tile_pool(name="keep", bufs=1))
+        stage = ctx.enter_context(tc.tile_pool(name="stage", bufs=5))
+        psum = ctx.enter_context(tc.psum_pool(name="psum", bufs=1))
+        ctx.enter_context(tc.manual_schedule())
+
+        formats = {"x": E4M3X4, "xt": E4M3X4, "g": E5M2X4, "gt": E5M2X4}
+        codes = {}
+        scales = {}
+        for name, width in (("g", M), ("gt", N), ("x", M), ("xt", N)):
+            codes[name] = keep.tile([P, PASSES, width], U32, name=name + "_codes", align_bytes=64)
+            scales[name] = keep.tile([P, PASSES, width], U8, name=name + "_scales", align_bytes=64)
+
+        def load(name, src, first, count, lo, width):
+            tile = raw.tile([P, count, PACK, width], F32, name="raw_%s_%d_%d" % (name, first, lo), align_bytes=64)
+            rows = src[first * K_PASS : (first + count) * K_PASS, lo : lo + width]
+            nc.sync.dma_start(out=tile[:], in_=rows.rearrange("(c p j) w -> p c j w", c=count, j=PACK))
+            return tile
+
+        def cast(src, vector_columns):
+            width = src.shape[2]
+            tile = stage.tile([P, HALF, PACK], BF16, name="grouped", align_bytes=64)
+            for copy, lo, hi in ((nc.scalar.copy, vector_columns, width), (nc.vector.tensor_copy, 0, vector_columns)):
+                if hi > lo:
+                    copy(
+                        out=tile[:, lo:hi, :].rearrange("p (b i) j -> p b j i", i=CAST_RUN),
+                        in_=src[:, :, lo:hi].rearrange("p j (b i) -> p b j i", i=CAST_RUN),
+                    )
+            return tile
+
+        def quantize(name, c, lo, width, grouped):
+            nc.vector.quantize_mx(
+                out=codes[name][:, c, lo : lo + width].bitcast(formats[name]),
+                scales=scales[name][:, c, lo : lo + width],
+                in_=grouped[:, 0:width, :].rearrange("p w j -> p (w j)"),
+            )
+
+        def multiply(acc, stationary, moving, c, m, lo, width):
+            rows = slice(m * P, (m + 1) * P)
+            cols = slice(lo, lo + width)
+            nc.tensor.matmul_mx(
+                out=acc[:, 0:width],
+                lhsT=codes[stationary][:, c, rows].bitcast(formats[stationary]),
+                lhsT_scale=scales[stationary][:, c, rows],
+                rhs=codes[moving][:, c, cols].bitcast(formats[moving]),
+                rhs_scale=scales[moving][:, c, cols],
+                start=(c == 0),
+                stop=(c == PASSES - 1),
+            )
+
+        g_first = load("g", g, 0, 1, 0, M)
+        gt_raw = [load("gt", gt, 0, 1, 0, N)]
+        g_rest = load("g", g, 1, PASSES - 1, 0, M)
+        gt_raw += [load("gt", gt, c, 1, 0, N) for c in range(1, PASSES)]
+        x_raw = load("x", x, 0, PASSES, 0, M)
+        xt_first = load("xt", xt, 0, 1, 0, N)
+        xt_raw = {(0, c): load("xt", xt, c, 1, *STRIPS[0]) for c in range(1, PASSES)}
+        r_sb = keep.tile([P, M_TILES, N], F32, name="r_sb", align_bytes=64)
+        r_rows = r.rearrange("(m p) n -> p m n", p=P)
+        out_rows = out.rearrange("(m p) n -> p m n", p=P)
+        for s in (1, 2):
+            for c in range(1, PASSES):
+                xt_raw[s, c] = load("xt", xt, c, 1, *STRIPS[s])
+            r_cols = slice((s - 1) * HALF, s * HALF)
+            nc.sync.dma_start(out=r_sb[:, :, r_cols], in_=r_rows[:, :, r_cols])
+        u_sb = keep.tile([P, M_TILES, N], F32, name="u_sb", align_bytes=64)
+        y_sb = keep.tile([P, M_TILES, N], F32, name="y_sb", align_bytes=64)
+
+        u_acc = [[psum.tile([P, HALF], F32, name="bank%d" % (2 * m + h)) for h in range(2)] for m in range(M_TILES)]
+
+        def prepare_narrow(name, tile, first, count):
+            grouped = [cast(tile[:, i], M // 2) for i in range(count)]
+            for i in range(count):
+                quantize(name, first + i, 0, M, grouped[i])
+
+        prepare_narrow("g", g_first, 0, 1)
+        for c in range(PASSES):
+            grouped = [cast(gt_raw[c][:, 0, :, h * HALF : (h + 1) * HALF], HALF // 2) for h in range(2)]
+            for h in range(2):
+                quantize("gt", c, h * HALF, HALF, grouped[h])
+                for m in range(M_TILES):
+                    multiply(u_acc[m][h], "g", "gt", c, m, h * HALF, HALF)
+            if c == 0:
+                prepare_narrow("g", g_rest, 1, PASSES - 1)
+
+        prepare_narrow("x", x_raw, 0, PASSES)
+        a_acc = [[psum.tile([P, HALF], F32, name="bank%d" % bank) for bank in banks] for banks in ((4, 5), (6, 7), (0, 2))]
+
+        def keep_u(m, h):
+            nc.scalar.copy(out=u_sb[:, m, h * HALF : (h + 1) * HALF], in_=u_acc[m][h][:])
+
+        def multiply_strip(s, c):
+            lo, width = STRIPS[s]
+            for m in range(M_TILES):
+                multiply(a_acc[s][m], "x", "xt", c, m, lo, width)
+
+        def quantize_strip(s, c, grouped_strip):
+            lo, width = STRIPS[s]
+            quantize("xt", c, lo, width, grouped_strip)
+            multiply_strip(s, c)
+
+        def product(s, m):
+            lo, width = STRIPS[s]
+            cols = slice(lo, lo + width)
+            nc.vector.tensor_tensor(out=y_sb[:, m, cols], in0=a_acc[s][m][:, 0:width], in1=u_sb[:, m, cols], op=MULT)
+
+        def finish(s, m):
+            lo, width = STRIPS[s]
+            cols = slice(lo, lo + width)
+            nc.vector.tensor_tensor(out=y_sb[:, m, cols], in0=y_sb[:, m, cols], in1=r_sb[:, m, cols], op=ADD)
+            nc.sync.dma_start(out=out_rows[:, m, cols], in_=y_sb[:, m, cols])
+
+        keep_u(0, 0)
+        grouped = [cast(xt_first[:, 0, :, h * HALF : (h + 1) * HALF], 320) for h in range(2)]
+        keep_u(1, 0)
+        for h in range(2):
+            quantize("xt", 0, h * HALF, HALF, grouped[h])
+        for s in range(len(STRIPS)):
+            multiply_strip(s, 0)
+        grouped = cast(xt_raw[0, 1][:, 0], 320)
+        keep_u(0, 1)
+        quantize_strip(0, 1, grouped)
+        grouped = cast(xt_raw[0, 2][:, 0], 384)
+        keep_u(1, 1)
+        quantize_strip(0, 2, grouped)
+
+        grouped = cast(xt_raw[1, 1][:, 0], 0)
+        for m in range(M_TILES):
+            product(0, m)
+        quantize_strip(1, 1, grouped)
+        quantize_strip(1, 2, cast(xt_raw[1, 2][:, 0], 0))
+        for m in range(M_TILES):
+            finish(0, m)
+            product(1, m)
+
+        grouped = [cast(xt_raw[2, 1][:, 0], 0), cast(xt_raw[2, 2][:, 0], 128)]
+        for c in range(1, PASSES):
+            quantize_strip(2, c, grouped[c - 1])
+        for m in range(M_TILES):
+            finish(1, m)
+        for m in range(M_TILES):
+            product(2, m)
+        for m in range(M_TILES):
+            finish(2, m)

@@ -22,7 +22,8 @@ CAST_RUN = 4
 M_TILES = M // P
 HALF = N // 2
 
-STRIPS = ((0, HALF), (HALF, HALF // 2), (HALF + HALF // 2, HALF // 2))
+WIDE, MIDDLE, NARROW, LAST = (0, 512), (512, 256), (768, 128), (896, 128)
+BOTH_NARROW = (768, 256)
 
 
 def tile_mix_ghost_res_kernel(tc, x, xt, g, gt, r, out):
@@ -30,7 +31,7 @@ def tile_mix_ghost_res_kernel(tc, x, xt, g, gt, r, out):
     with ExitStack() as ctx:
         raw = ctx.enter_context(tc.tile_pool(name="raw", bufs=1))
         keep = ctx.enter_context(tc.tile_pool(name="keep", bufs=1))
-        stage = ctx.enter_context(tc.tile_pool(name="stage", bufs=5))
+        stage = ctx.enter_context(tc.tile_pool(name="stage", bufs=8))
         psum = ctx.enter_context(tc.psum_pool(name="psum", bufs=1))
         ctx.enter_context(tc.manual_schedule())
 
@@ -84,15 +85,27 @@ def tile_mix_ghost_res_kernel(tc, x, xt, g, gt, r, out):
         gt_raw += [load("gt", gt, c, 1, 0, N) for c in range(1, PASSES)]
         x_raw = load("x", x, 0, PASSES, 0, M)
         xt_first = load("xt", xt, 0, 1, 0, N)
-        xt_raw = {(0, c): load("xt", xt, c, 1, *STRIPS[0]) for c in range(1, PASSES)}
+        xt_raw = {}
         r_sb = keep.tile([P, M_TILES, N], F32, name="r_sb", align_bytes=64)
         r_rows = r.rearrange("(m p) n -> p m n", p=P)
         out_rows = out.rearrange("(m p) n -> p m n", p=P)
-        for s in (1, 2):
+
+        def load_xt(c, strip):
+            xt_raw[c, strip] = load("xt", xt, c, 1, *strip)[:, 0]
+
+        def load_r(strip):
+            cols = slice(strip[0], strip[0] + strip[1])
+            nc.sync.dma_start(out=r_sb[:, :, cols], in_=r_rows[:, :, cols])
+
+        for strip in (WIDE, MIDDLE):
             for c in range(1, PASSES):
-                xt_raw[s, c] = load("xt", xt, c, 1, *STRIPS[s])
-            r_cols = slice((s - 1) * HALF, s * HALF)
-            nc.sync.dma_start(out=r_sb[:, :, r_cols], in_=r_rows[:, :, r_cols])
+                load_xt(c, strip)
+        load_r(WIDE)
+        load_xt(1, BOTH_NARROW)
+        load_xt(2, NARROW)
+        load_xt(2, LAST)
+        load_r(MIDDLE)
+        load_r(BOTH_NARROW)
         u_sb = keep.tile([P, M_TILES, N], F32, name="u_sb", align_bytes=64)
         y_sb = keep.tile([P, M_TILES, N], F32, name="y_sb", align_bytes=64)
 
@@ -114,61 +127,79 @@ def tile_mix_ghost_res_kernel(tc, x, xt, g, gt, r, out):
                 prepare_narrow("g", g_rest, 1, PASSES - 1)
 
         prepare_narrow("x", x_raw, 0, PASSES)
-        a_acc = [[psum.tile([P, HALF], F32, name="bank%d" % bank) for bank in banks] for banks in ((4, 5), (6, 7), (0, 2))]
 
-        def keep_u(m, h):
-            nc.scalar.copy(out=u_sb[:, m, h * HALF : (h + 1) * HALF], in_=u_acc[m][h][:])
-
-        def multiply_strip(s, c):
-            lo, width = STRIPS[s]
+        for h in range(2):
             for m in range(M_TILES):
-                multiply(a_acc[s][m], "x", "xt", c, m, lo, width)
+                nc.scalar.copy(out=u_sb[:, m, h * HALF : (h + 1) * HALF], in_=u_acc[m][h][:])
 
-        def quantize_strip(s, c, grouped_strip):
-            lo, width = STRIPS[s]
-            quantize("xt", c, lo, width, grouped_strip)
-            multiply_strip(s, c)
+        a_acc = {
+            strip: [psum.tile([P, HALF], F32, name="bank%d" % bank) for bank in banks]
+            for strip, banks in ((WIDE, (4, 5)), (MIDDLE, (6, 7)), (NARROW, (0, 2)), (LAST, (1, 3)))
+        }
 
-        def product(s, m):
-            lo, width = STRIPS[s]
+        def cast_xt(c, strip, vector_columns):
+            return cast(xt_raw[c, strip], vector_columns)
+
+        def quantize_xt(c, strip, grouped_strip):
+            quantize("xt", c, strip[0], strip[1], grouped_strip)
+
+        def multiply_strip(c, strip):
+            for m in range(M_TILES):
+                multiply(a_acc[strip][m], "x", "xt", c, m, *strip)
+
+        def product(strip, m):
+            lo, width = strip
             cols = slice(lo, lo + width)
-            nc.vector.tensor_tensor(out=y_sb[:, m, cols], in0=a_acc[s][m][:, 0:width], in1=u_sb[:, m, cols], op=MULT)
+            nc.vector.tensor_tensor(out=y_sb[:, m, cols], in0=a_acc[strip][m][:, 0:width], in1=u_sb[:, m, cols], op=MULT)
 
-        def finish(s, m):
-            lo, width = STRIPS[s]
-            cols = slice(lo, lo + width)
-            nc.vector.tensor_tensor(out=y_sb[:, m, cols], in0=y_sb[:, m, cols], in1=r_sb[:, m, cols], op=ADD)
-            nc.sync.dma_start(out=out_rows[:, m, cols], in_=y_sb[:, m, cols])
+        def add_r(strip, groups):
+            cols = slice(strip[0], strip[0] + strip[1])
+            nc.vector.tensor_tensor(out=y_sb[:, groups, cols], in0=y_sb[:, groups, cols], in1=r_sb[:, groups, cols], op=ADD)
 
-        keep_u(0, 0)
+        def store(strip, groups):
+            cols = slice(strip[0], strip[0] + strip[1])
+            nc.sync.dma_start(out=out_rows[:, groups, cols], in_=y_sb[:, groups, cols])
+
+        first, second, both = slice(0, 1), slice(1, 2), slice(0, M_TILES)
+
         grouped = [cast(xt_first[:, 0, :, h * HALF : (h + 1) * HALF], 320) for h in range(2)]
-        keep_u(1, 0)
         for h in range(2):
             quantize("xt", 0, h * HALF, HALF, grouped[h])
-        for s in range(len(STRIPS)):
-            multiply_strip(s, 0)
-        grouped = cast(xt_raw[0, 1][:, 0], 320)
-        keep_u(0, 1)
-        quantize_strip(0, 1, grouped)
-        grouped = cast(xt_raw[0, 2][:, 0], 384)
-        keep_u(1, 1)
-        quantize_strip(0, 2, grouped)
-
-        grouped = cast(xt_raw[1, 1][:, 0], 0)
-        for m in range(M_TILES):
-            product(0, m)
-        quantize_strip(1, 1, grouped)
-        quantize_strip(1, 2, cast(xt_raw[1, 2][:, 0], 0))
-        for m in range(M_TILES):
-            finish(0, m)
-            product(1, m)
-
-        grouped = [cast(xt_raw[2, 1][:, 0], 0), cast(xt_raw[2, 2][:, 0], 128)]
+        multiply_strip(0, WIDE)
         for c in range(1, PASSES):
-            quantize_strip(2, c, grouped[c - 1])
-        for m in range(M_TILES):
-            finish(1, m)
-        for m in range(M_TILES):
-            product(2, m)
-        for m in range(M_TILES):
-            finish(2, m)
+            quantize_xt(c, WIDE, cast_xt(c, WIDE, 320))
+            multiply_strip(c, WIDE)
+
+        quantize_xt(1, MIDDLE, cast_xt(1, MIDDLE, 128))
+        multiply_strip(0, MIDDLE)
+        multiply_strip(1, MIDDLE)
+        grouped = cast_xt(2, MIDDLE, 0)
+        product(WIDE, 0)
+        product(WIDE, 1)
+        add_r(WIDE, first)
+        quantize_xt(2, MIDDLE, grouped)
+        multiply_strip(2, MIDDLE)
+        multiply_strip(0, NARROW)
+        multiply_strip(0, LAST)
+        add_r(WIDE, second)
+
+        grouped = cast_xt(1, BOTH_NARROW, 128)
+        product(MIDDLE, 0)
+        quantize_xt(1, BOTH_NARROW, grouped)
+        multiply_strip(1, NARROW)
+        multiply_strip(1, LAST)
+        product(MIDDLE, 1)
+
+        grouped = {NARROW: cast_xt(2, NARROW, 0), LAST: cast_xt(2, LAST, 80)}
+        for strip in (NARROW, LAST):
+            quantize_xt(2, strip, grouped[strip])
+            multiply_strip(2, strip)
+        store(WIDE, both)
+        add_r(MIDDLE, both)
+        store(MIDDLE, both)
+        for strip in (NARROW, LAST):
+            for m in range(M_TILES):
+                product(strip, m)
+        for strip in (NARROW, LAST):
+            add_r(strip, both)
+            store(strip, both)

@@ -22,8 +22,8 @@ CAST_RUN = 4
 M_TILES = M // P
 HALF = N // 2
 
-WIDE, MIDDLE, NARROW, LAST = (0, 512), (512, 256), (768, 128), (896, 128)
-BOTH_NARROW = (768, 256)
+STRIP = 256
+STRIPS = N // STRIP
 
 
 def tile_mix_ghost_res_kernel(tc, x, xt, g, gt, r, out):
@@ -83,29 +83,17 @@ def tile_mix_ghost_res_kernel(tc, x, xt, g, gt, r, out):
         gt_raw = [load("gt", gt, 0, 1, 0, N)]
         g_rest = load("g", g, 1, PASSES - 1, 0, M)
         gt_raw += [load("gt", gt, c, 1, 0, N) for c in range(1, PASSES)]
-        x_raw = load("x", x, 0, PASSES, 0, M)
-        xt_first = load("xt", xt, 0, 1, 0, N)
-        xt_raw = {}
+        x_first = load("x", x, 0, PASSES - 1, 0, M)
+        xt_whole = [load("xt", xt, c, 1, 0, N)[:, 0] for c in range(PASSES - 1)]
+        x_last = load("x", x, PASSES - 1, 1, 0, M)
+        xt_wide = load("xt", xt, PASSES - 1, 1, 0, HALF)[:, 0]
+        xt_last = [xt_wide[:, :, 0:STRIP], xt_wide[:, :, STRIP:HALF]]
+        xt_last += [load("xt", xt, PASSES - 1, 1, s * STRIP, STRIP)[:, 0] for s in range(2, STRIPS)]
         r_sb = keep.tile([P, M_TILES, N], F32, name="r_sb", align_bytes=64)
         r_rows = r.rearrange("(m p) n -> p m n", p=P)
         out_rows = out.rearrange("(m p) n -> p m n", p=P)
-
-        def load_xt(c, strip):
-            xt_raw[c, strip] = load("xt", xt, c, 1, *strip)[:, 0]
-
-        def load_r(strip):
-            cols = slice(strip[0], strip[0] + strip[1])
-            nc.sync.dma_start(out=r_sb[:, :, cols], in_=r_rows[:, :, cols])
-
-        for strip in (WIDE, MIDDLE):
-            for c in range(1, PASSES):
-                load_xt(c, strip)
-        load_r(WIDE)
-        load_xt(1, BOTH_NARROW)
-        load_xt(2, NARROW)
-        load_xt(2, LAST)
-        load_r(MIDDLE)
-        load_r(BOTH_NARROW)
+        for m in range(M_TILES):
+            nc.sync.dma_start(out=r_sb[:, m, :], in_=r_rows[:, m, :])
         u_sb = keep.tile([P, M_TILES, N], F32, name="u_sb", align_bytes=64)
         y_sb = keep.tile([P, M_TILES, N], F32, name="y_sb", align_bytes=64)
 
@@ -126,80 +114,65 @@ def tile_mix_ghost_res_kernel(tc, x, xt, g, gt, r, out):
             if c == 0:
                 prepare_narrow("g", g_rest, 1, PASSES - 1)
 
-        prepare_narrow("x", x_raw, 0, PASSES)
+        prepare_narrow("x", x_first, 0, PASSES - 1)
 
         for h in range(2):
             for m in range(M_TILES):
                 nc.scalar.copy(out=u_sb[:, m, h * HALF : (h + 1) * HALF], in_=u_acc[m][h][:])
 
-        a_acc = {
-            strip: [psum.tile([P, HALF], F32, name="bank%d" % bank) for bank in banks]
-            for strip, banks in ((WIDE, (4, 5)), (MIDDLE, (6, 7)), (NARROW, (0, 2)), (LAST, (1, 3)))
-        }
+        a_acc = [[psum.tile([P, HALF], F32, name="bank%d" % bank) for bank in banks] for banks in ((4, 5), (6, 7), (0, 2), (1, 3))]
 
-        def cast_xt(c, strip, vector_columns):
-            return cast(xt_raw[c, strip], vector_columns)
-
-        def quantize_xt(c, strip, grouped_strip):
-            quantize("xt", c, strip[0], strip[1], grouped_strip)
-
-        def multiply_strip(c, strip):
+        def multiply_strip(c, s):
             for m in range(M_TILES):
-                multiply(a_acc[strip][m], "x", "xt", c, m, *strip)
+                multiply(a_acc[s][m], "x", "xt", c, m, s * STRIP, STRIP)
 
-        def product(strip, m):
-            lo, width = strip
-            cols = slice(lo, lo + width)
-            nc.vector.tensor_tensor(out=y_sb[:, m, cols], in0=a_acc[strip][m][:, 0:width], in1=u_sb[:, m, cols], op=MULT)
+        def quantize_strip(c, s, grouped_strip):
+            quantize("xt", c, s * STRIP, STRIP, grouped_strip)
+            multiply_strip(c, s)
 
-        def add_r(strip, groups):
-            cols = slice(strip[0], strip[0] + strip[1])
-            nc.vector.tensor_tensor(out=y_sb[:, groups, cols], in0=y_sb[:, groups, cols], in1=r_sb[:, groups, cols], op=ADD)
+        def product(m, s):
+            cols = slice(s * STRIP, (s + 1) * STRIP)
+            nc.vector.tensor_tensor(out=y_sb[:, m, cols], in0=a_acc[s][m][:, 0:STRIP], in1=u_sb[:, m, cols], op=MULT)
 
-        def store(strip, groups):
-            cols = slice(strip[0], strip[0] + strip[1])
-            nc.sync.dma_start(out=out_rows[:, groups, cols], in_=y_sb[:, groups, cols])
+        def finish(m, first, count):
+            cols = slice(first * STRIP, (first + count) * STRIP)
+            nc.vector.tensor_tensor(out=y_sb[:, m, cols], in0=y_sb[:, m, cols], in1=r_sb[:, m, cols], op=ADD)
+            nc.sync.dma_start(out=out_rows[:, m, cols], in_=y_sb[:, m, cols])
 
-        first, second, both = slice(0, 1), slice(1, 2), slice(0, M_TILES)
-
-        grouped = [cast(xt_first[:, 0, :, h * HALF : (h + 1) * HALF], 320) for h in range(2)]
+        grouped = [cast(xt_whole[0][:, :, h * HALF : (h + 1) * HALF], 320) for h in range(2)]
         for h in range(2):
             quantize("xt", 0, h * HALF, HALF, grouped[h])
-        multiply_strip(0, WIDE)
-        for c in range(1, PASSES):
-            quantize_xt(c, WIDE, cast_xt(c, WIDE, 320))
-            multiply_strip(c, WIDE)
+        for s in range(STRIPS):
+            multiply_strip(0, s)
 
-        quantize_xt(1, MIDDLE, cast_xt(1, MIDDLE, 128))
-        multiply_strip(0, MIDDLE)
-        multiply_strip(1, MIDDLE)
-        grouped = cast_xt(2, MIDDLE, 0)
-        product(WIDE, 0)
-        product(WIDE, 1)
-        add_r(WIDE, first)
-        quantize_xt(2, MIDDLE, grouped)
-        multiply_strip(2, MIDDLE)
-        multiply_strip(0, NARROW)
-        multiply_strip(0, LAST)
-        add_r(WIDE, second)
+        grouped = []
+        for s in range(STRIPS):
+            grouped.append(cast(xt_whole[1][:, :, s * STRIP : (s + 1) * STRIP], 144))
+            if s > 0:
+                quantize_strip(1, s - 1, grouped[s - 1])
+        grouped_x = cast(x_last[:, 0], M // 2)
+        quantize_strip(1, STRIPS - 1, grouped[STRIPS - 1])
+        quantize("x", PASSES - 1, 0, M, grouped_x)
 
-        grouped = cast_xt(1, BOTH_NARROW, 128)
-        product(MIDDLE, 0)
-        quantize_xt(1, BOTH_NARROW, grouped)
-        multiply_strip(1, NARROW)
-        multiply_strip(1, LAST)
-        product(MIDDLE, 1)
-
-        grouped = {NARROW: cast_xt(2, NARROW, 0), LAST: cast_xt(2, LAST, 80)}
-        for strip in (NARROW, LAST):
-            quantize_xt(2, strip, grouped[strip])
-            multiply_strip(2, strip)
-        store(WIDE, both)
-        add_r(MIDDLE, both)
-        store(MIDDLE, both)
-        for strip in (NARROW, LAST):
-            for m in range(M_TILES):
-                product(strip, m)
-        for strip in (NARROW, LAST):
-            add_r(strip, both)
-            store(strip, both)
+        last = PASSES - 1
+        grouped = [cast(xt_last[0], 192), cast(xt_last[1], 128)]
+        quantize_strip(last, 0, grouped[0])
+        quantize_strip(last, 1, grouped[1])
+        grouped = cast(xt_last[2], 160)
+        product(0, 0)
+        quantize_strip(last, 2, grouped)
+        product(0, 1)
+        product(1, 0)
+        grouped = cast(xt_last[3], 0)
+        product(1, 1)
+        product(0, 2)
+        product(1, 2)
+        finish(0, 0, 1)
+        quantize_strip(last, 3, grouped)
+        finish(0, 1, 2)
+        finish(1, 0, 2)
+        product(0, 3)
+        finish(1, 2, 1)
+        product(1, 3)
+        finish(0, 3, 1)
+        finish(1, 3, 1)

@@ -42,10 +42,10 @@ def tile_mix_ghost_res_kernel(tc, x, xt, g, gt, r, out):
             codes[name] = keep.tile([P, PASSES, width], U32, name=name + "_codes", align_bytes=64)
             scales[name] = keep.tile([P, PASSES, width], U8, name=name + "_scales", align_bytes=64)
 
-        def load(name, src, first, count, lo, width):
-            tile = raw.tile([P, count, PACK, width], F32, name="raw_%s_%d_%d" % (name, first, lo), align_bytes=64)
-            rows = src[first * K_PASS : (first + count) * K_PASS, lo : lo + width]
-            nc.sync.dma_start(out=tile[:], in_=rows.rearrange("(c p j) w -> p c j w", c=count, j=PACK))
+        def load(name, src, c, lo, width):
+            tile = raw.tile([P, PACK, width], F32, name="raw_%s_%d_%d" % (name, c, lo), align_bytes=64)
+            rows = src[c * K_PASS : (c + 1) * K_PASS, lo : lo + width]
+            nc.sync.dma_start(out=tile[:], in_=rows.rearrange("(p j) w -> p j w", j=PACK))
             return tile
 
         def cast(src, vector_columns):
@@ -79,16 +79,18 @@ def tile_mix_ghost_res_kernel(tc, x, xt, g, gt, r, out):
                 stop=(c == PASSES - 1),
             )
 
-        g_first = load("g", g, 0, 1, 0, M)
-        gt_raw = [load("gt", gt, 0, 1, 0, N)]
-        g_rest = load("g", g, 1, PASSES - 1, 0, M)
-        gt_raw += [load("gt", gt, c, 1, 0, N) for c in range(1, PASSES)]
-        x_first = load("x", x, 0, PASSES - 1, 0, M)
-        xt_whole = [load("xt", xt, c, 1, 0, N)[:, 0] for c in range(PASSES - 1)]
-        x_last = load("x", x, PASSES - 1, 1, 0, M)
-        xt_wide = load("xt", xt, PASSES - 1, 1, 0, HALF)[:, 0]
+        last = PASSES - 1
+        g_raw, gt_raw, x_raw, xt_whole = [], [], [], []
+        for c in range(PASSES):
+            g_raw.append(load("g", g, c, 0, M))
+            gt_raw.append(load("gt", gt, c, 0, N))
+        for c in range(last):
+            x_raw.append(load("x", x, c, 0, M))
+            xt_whole.append(load("xt", xt, c, 0, N))
+        x_raw.append(load("x", x, last, 0, M))
+        xt_wide = load("xt", xt, last, 0, HALF)
         xt_last = [xt_wide[:, :, 0:STRIP], xt_wide[:, :, STRIP:HALF]]
-        xt_last += [load("xt", xt, PASSES - 1, 1, s * STRIP, STRIP)[:, 0] for s in range(2, STRIPS)]
+        xt_last += [load("xt", xt, last, s * STRIP, STRIP)[:] for s in range(2, STRIPS)]
         r_sb = keep.tile([P, M_TILES, N], F32, name="r_sb", align_bytes=64)
         r_rows = r.rearrange("(m p) n -> p m n", p=P)
         out_rows = out.rearrange("(m p) n -> p m n", p=P)
@@ -99,22 +101,15 @@ def tile_mix_ghost_res_kernel(tc, x, xt, g, gt, r, out):
 
         u_acc = [[psum.tile([P, HALF], F32, name="bank%d" % (2 * m + h)) for h in range(2)] for m in range(M_TILES)]
 
-        def prepare_narrow(name, tile, first, count):
-            grouped = [cast(tile[:, i], M // 2) for i in range(count)]
-            for i in range(count):
-                quantize(name, first + i, 0, M, grouped[i])
-
-        prepare_narrow("g", g_first, 0, 1)
         for c in range(PASSES):
-            grouped = [cast(gt_raw[c][:, 0, :, h * HALF : (h + 1) * HALF], HALF // 2) for h in range(2)]
+            quantize("g", c, 0, M, cast(g_raw[c][:], M // 2))
+            grouped = [cast(gt_raw[c][:, :, h * HALF : (h + 1) * HALF], 320) for h in range(2)]
             for h in range(2):
                 quantize("gt", c, h * HALF, HALF, grouped[h])
                 for m in range(M_TILES):
                     multiply(u_acc[m][h], "g", "gt", c, m, h * HALF, HALF)
-            if c == 0:
-                prepare_narrow("g", g_rest, 1, PASSES - 1)
 
-        prepare_narrow("x", x_first, 0, PASSES - 1)
+        quantize("x", 0, 0, M, cast(x_raw[0][:], M // 2))
 
         for h in range(2):
             for m in range(M_TILES):
@@ -145,16 +140,16 @@ def tile_mix_ghost_res_kernel(tc, x, xt, g, gt, r, out):
         for s in range(STRIPS):
             multiply_strip(0, s)
 
+        quantize("x", 1, 0, M, cast(x_raw[1][:], M // 2))
         grouped = []
         for s in range(STRIPS):
             grouped.append(cast(xt_whole[1][:, :, s * STRIP : (s + 1) * STRIP], 144))
             if s > 0:
                 quantize_strip(1, s - 1, grouped[s - 1])
-        grouped_x = cast(x_last[:, 0], M // 2)
+        grouped_x = cast(x_raw[last][:], M // 2)
         quantize_strip(1, STRIPS - 1, grouped[STRIPS - 1])
         quantize("x", PASSES - 1, 0, M, grouped_x)
 
-        last = PASSES - 1
         grouped = [cast(xt_last[0], 192), cast(xt_last[1], 128)]
         quantize_strip(last, 0, grouped[0])
         quantize_strip(last, 1, grouped[1])

@@ -94,8 +94,8 @@ def tile_mix_ghost_res_kernel(tc, x, xt, g, gt, r, out):
         r_sb = keep.tile([P, M_TILES, N], F32, name="r_sb", align_bytes=64)
         r_rows = r.rearrange("(m p) n -> p m n", p=P)
         out_rows = out.rearrange("(m p) n -> p m n", p=P)
-        for m in range(M_TILES):
-            nc.sync.dma_start(out=r_sb[:, m, :], in_=r_rows[:, m, :])
+        for m, cols in ((0, slice(0, HALF)), (1, slice(0, N)), (0, slice(HALF, N))):
+            nc.sync.dma_start(out=r_sb[:, m, cols], in_=r_rows[:, m, cols])
         u_sb = keep.tile([P, M_TILES, N], F32, name="u_sb", align_bytes=64)
         y_sb = keep.tile([P, M_TILES, N], F32, name="y_sb", align_bytes=64)
 
@@ -118,7 +118,7 @@ def tile_mix_ghost_res_kernel(tc, x, xt, g, gt, r, out):
         a_acc = [[psum.tile([P, HALF], F32, name="bank%d" % bank) for bank in banks] for banks in ((4, 5), (6, 7), (0, 2), (1, 3))]
 
         def multiply_strip(c, s):
-            for m in range(M_TILES):
+            for m in reversed(range(M_TILES)):
                 multiply(a_acc[s][m], "x", "xt", c, m, s * STRIP, STRIP)
 
         def quantize_strip(c, s, grouped_strip):
@@ -129,9 +129,9 @@ def tile_mix_ghost_res_kernel(tc, x, xt, g, gt, r, out):
             cols = slice(s * STRIP, (s + 1) * STRIP)
             nc.vector.tensor_tensor(out=y_sb[:, m, cols], in0=a_acc[s][m][:, 0:STRIP], in1=u_sb[:, m, cols], op=MULT)
 
-        def finish(m, first, count):
+        def finish(m, first, count, engine=nc.vector):
             cols = slice(first * STRIP, (first + count) * STRIP)
-            nc.vector.tensor_tensor(out=y_sb[:, m, cols], in0=y_sb[:, m, cols], in1=r_sb[:, m, cols], op=ADD)
+            engine.tensor_tensor(out=y_sb[:, m, cols], in0=y_sb[:, m, cols], in1=r_sb[:, m, cols], op=ADD)
             nc.sync.dma_start(out=out_rows[:, m, cols], in_=y_sb[:, m, cols])
 
         grouped = [cast(xt_whole[0][:, :, h * HALF : (h + 1) * HALF], 320) for h in range(2)]
@@ -154,20 +154,21 @@ def tile_mix_ghost_res_kernel(tc, x, xt, g, gt, r, out):
         quantize_strip(last, 0, grouped[0])
         quantize_strip(last, 1, grouped[1])
         grouped = cast(xt_last[2], 160)
-        product(0, 0)
-        quantize_strip(last, 2, grouped)
-        product(0, 1)
         product(1, 0)
-        grouped = cast(xt_last[3], 0)
+        quantize_strip(last, 2, grouped)
         product(1, 1)
-        product(0, 2)
+        product(0, 0)
+        grouped = cast(xt_last[3], 0)
+        finish(0, 0, 1, nc.gpsimd)
+        product(0, 1)
         product(1, 2)
-        finish(0, 0, 1)
+        product(0, 2)
+        finish(0, 1, 1)
         quantize_strip(last, 3, grouped)
-        finish(0, 1, 2)
         finish(1, 0, 2)
-        product(0, 3)
         finish(1, 2, 1)
+        finish(0, 2, 1)
         product(1, 3)
-        finish(0, 3, 1)
+        product(0, 3)
         finish(1, 3, 1)
+        finish(0, 3, 1)

@@ -18,12 +18,18 @@ P = 128
 PACK = 4
 K_PASS = P * PACK
 PASSES = K // K_PASS
+LAST = PASSES - 1
 CAST_RUN = 4
 M_TILES = M // P
 HALF = N // 2
 
 STRIP = 256
 STRIPS = N // STRIP
+
+VECTOR_OF_HALF = 320
+VECTOR_OF_STRIP = 160
+VECTOR_OF_NARROW = M // 2
+VECTOR_OF_LAST = (160, 128, 128, 0)
 
 
 def tile_mix_ghost_res_kernel(tc, x, xt, g, gt, r, out):
@@ -76,21 +82,20 @@ def tile_mix_ghost_res_kernel(tc, x, xt, g, gt, r, out):
                 rhs=codes[moving][:, c, cols].bitcast(formats[moving]),
                 rhs_scale=scales[moving][:, c, cols],
                 start=(c == 0),
-                stop=(c == PASSES - 1),
+                stop=(c == LAST),
             )
 
-        last = PASSES - 1
         g_raw, gt_raw, x_raw, xt_whole = [], [], [], []
         for c in range(PASSES):
             g_raw.append(load("g", g, c, 0, M))
             gt_raw.append(load("gt", gt, c, 0, N))
-        for c in range(last):
+        for c in range(LAST):
             x_raw.append(load("x", x, c, 0, M))
             xt_whole.append(load("xt", xt, c, 0, N))
-        x_raw.append(load("x", x, last, 0, M))
-        xt_wide = load("xt", xt, last, 0, HALF)
+        x_raw.append(load("x", x, LAST, 0, M))
+        xt_wide = load("xt", xt, LAST, 0, HALF)
         xt_last = [xt_wide[:, :, 0:STRIP], xt_wide[:, :, STRIP:HALF]]
-        xt_last += [load("xt", xt, last, s * STRIP, STRIP)[:] for s in range(2, STRIPS)]
+        xt_last += [load("xt", xt, LAST, s * STRIP, STRIP)[:] for s in range(2, STRIPS)]
         r_sb = keep.tile([P, M_TILES, N], F32, name="r_sb", align_bytes=64)
         r_rows = r.rearrange("(m p) n -> p m n", p=P)
         out_rows = out.rearrange("(m p) n -> p m n", p=P)
@@ -100,16 +105,15 @@ def tile_mix_ghost_res_kernel(tc, x, xt, g, gt, r, out):
         y_sb = keep.tile([P, M_TILES, N], F32, name="y_sb", align_bytes=64)
 
         u_acc = [[psum.tile([P, HALF], F32, name="bank%d" % (2 * m + h)) for h in range(2)] for m in range(M_TILES)]
-
         for c in range(PASSES):
-            quantize("g", c, 0, M, cast(g_raw[c][:], M // 2))
-            grouped = [cast(gt_raw[c][:, :, h * HALF : (h + 1) * HALF], 320) for h in range(2)]
+            quantize("g", c, 0, M, cast(g_raw[c][:], VECTOR_OF_NARROW))
+            grouped = [cast(gt_raw[c][:, :, h * HALF : (h + 1) * HALF], VECTOR_OF_HALF) for h in range(2)]
             for h in range(2):
                 quantize("gt", c, h * HALF, HALF, grouped[h])
                 for m in range(M_TILES):
                     multiply(u_acc[m][h], "g", "gt", c, m, h * HALF, HALF)
 
-        quantize("x", 0, 0, M, cast(x_raw[0][:], M // 2))
+        quantize("x", 0, 0, M, cast(x_raw[0][:], VECTOR_OF_NARROW))
 
         for h in range(2):
             for m in range(M_TILES):
@@ -129,46 +133,46 @@ def tile_mix_ghost_res_kernel(tc, x, xt, g, gt, r, out):
             cols = slice(s * STRIP, (s + 1) * STRIP)
             nc.vector.tensor_tensor(out=y_sb[:, m, cols], in0=a_acc[s][m][:, 0:STRIP], in1=u_sb[:, m, cols], op=MULT)
 
-        def finish(m, first, count, engine=nc.vector):
+        def finish(m, first, count, engine):
             cols = slice(first * STRIP, (first + count) * STRIP)
             engine.tensor_tensor(out=y_sb[:, m, cols], in0=y_sb[:, m, cols], in1=r_sb[:, m, cols], op=ADD)
             nc.sync.dma_start(out=out_rows[:, m, cols], in_=y_sb[:, m, cols])
 
-        grouped = [cast(xt_whole[0][:, :, h * HALF : (h + 1) * HALF], 320) for h in range(2)]
+        grouped = [cast(xt_whole[0][:, :, h * HALF : (h + 1) * HALF], VECTOR_OF_HALF) for h in range(2)]
         for h in range(2):
             quantize("xt", 0, h * HALF, HALF, grouped[h])
         for s in range(STRIPS):
             multiply_strip(0, s)
 
-        quantize("x", 1, 0, M, cast(x_raw[1][:], M // 2))
+        quantize("x", 1, 0, M, cast(x_raw[1][:], VECTOR_OF_NARROW))
         grouped = []
         for s in range(STRIPS):
-            grouped.append(cast(xt_whole[1][:, :, s * STRIP : (s + 1) * STRIP], 144))
+            grouped.append(cast(xt_whole[1][:, :, s * STRIP : (s + 1) * STRIP], VECTOR_OF_STRIP))
             if s > 0:
                 quantize_strip(1, s - 1, grouped[s - 1])
-        grouped_x = cast(x_raw[last][:], M // 2)
+        grouped_x = cast(x_raw[LAST][:], VECTOR_OF_NARROW)
         quantize_strip(1, STRIPS - 1, grouped[STRIPS - 1])
-        quantize("x", PASSES - 1, 0, M, grouped_x)
+        quantize("x", LAST, 0, M, grouped_x)
 
-        grouped = [cast(xt_last[0], 192), cast(xt_last[1], 128)]
-        quantize_strip(last, 0, grouped[0])
-        quantize_strip(last, 1, grouped[1])
-        grouped = cast(xt_last[2], 160)
+        grouped = [cast(xt_last[s], VECTOR_OF_LAST[s]) for s in range(2)]
+        for s in range(2):
+            quantize_strip(LAST, s, grouped[s])
+        grouped = cast(xt_last[2], VECTOR_OF_LAST[2])
         product(1, 0)
-        quantize_strip(last, 2, grouped)
+        quantize_strip(LAST, 2, grouped)
         product(1, 1)
         product(0, 0)
-        grouped = cast(xt_last[3], 0)
+        grouped = cast(xt_last[3], VECTOR_OF_LAST[3])
         finish(0, 0, 1, nc.gpsimd)
         product(0, 1)
         product(1, 2)
         product(0, 2)
-        finish(0, 1, 1)
-        quantize_strip(last, 3, grouped)
-        finish(1, 0, 2)
-        finish(1, 2, 1)
-        finish(0, 2, 1)
-        product(1, 3)
-        product(0, 3)
-        finish(1, 3, 1)
-        finish(0, 3, 1)
+        finish(0, 1, 1, nc.vector)
+        quantize_strip(LAST, 3, grouped)
+        finish(1, 0, 2, nc.vector)
+        finish(1, 2, 1, nc.vector)
+        finish(0, 2, 1, nc.vector)
+        for m in reversed(range(M_TILES)):
+            product(m, 3)
+        for m in reversed(range(M_TILES)):
+            finish(m, 3, 1, nc.vector)

@@ -21,6 +21,7 @@ PASSES = K // K_PASS
 LAST = PASSES - 1
 CAST_RUN = 4
 M_TILES = M // P
+DMA_ALIGN = 256
 HALF = N // 2
 
 STRIP = 256
@@ -49,7 +50,7 @@ def tile_mix_ghost_res_kernel(tc, x, xt, g, gt, r, out):
             scales[name] = keep.tile([P, PASSES, width], U8, name=name + "_scales", align_bytes=64)
 
         def load(name, src, c, lo, width):
-            tile = raw.tile([P, PACK, width], F32, name="raw_%s_%d_%d" % (name, c, lo), align_bytes=64)
+            tile = raw.tile([P, PACK, width], F32, name="raw_%s_%d_%d" % (name, c, lo), align_bytes=DMA_ALIGN)
             rows = src[c * K_PASS : (c + 1) * K_PASS, lo : lo + width]
             nc.sync.dma_start(out=tile[:], in_=rows.rearrange("(p j) w -> p j w", j=PACK))
             return tile
@@ -96,13 +97,13 @@ def tile_mix_ghost_res_kernel(tc, x, xt, g, gt, r, out):
         xt_wide = load("xt", xt, LAST, 0, HALF)
         xt_last = [xt_wide[:, :, 0:STRIP], xt_wide[:, :, STRIP:HALF]]
         xt_last += [load("xt", xt, LAST, s * STRIP, STRIP)[:] for s in range(2, STRIPS)]
-        r_sb = keep.tile([P, M_TILES, N], F32, name="r_sb", align_bytes=64)
+        r_sb = keep.tile([P, M_TILES, N], F32, name="r_sb", align_bytes=DMA_ALIGN)
         r_rows = r.rearrange("(m p) n -> p m n", p=P)
         out_rows = out.rearrange("(m p) n -> p m n", p=P)
         for m, cols in ((0, slice(0, HALF)), (1, slice(0, N)), (0, slice(HALF, N))):
             nc.sync.dma_start(out=r_sb[:, m, cols], in_=r_rows[:, m, cols])
         u_sb = keep.tile([P, M_TILES, N], F32, name="u_sb", align_bytes=64)
-        y_sb = keep.tile([P, M_TILES, N], F32, name="y_sb", align_bytes=64)
+        y_sb = keep.tile([P, M_TILES, N], F32, name="y_sb", align_bytes=DMA_ALIGN)
 
         u_acc = [[psum.tile([P, HALF], F32, name="bank%d" % (2 * m + h)) for h in range(2)] for m in range(M_TILES)]
         for c in range(PASSES):

@@ -21,8 +21,10 @@ PASSES = K // K_PASS
 LAST = PASSES - 1
 CAST_RUN = 4
 M_TILES = M // P
-DMA_ALIGN = 256
 HALF = N // 2
+
+DMA_ALIGN = 256
+MX_ALIGN = 64
 
 STRIP = 256
 STRIPS = N // STRIP
@@ -30,7 +32,7 @@ STRIPS = N // STRIP
 VECTOR_OF_HALF = 320
 VECTOR_OF_STRIP = 160
 VECTOR_OF_NARROW = M // 2
-VECTOR_OF_LAST = (160, 128, 128, 0)
+VECTOR_OF_LAST = (160, 144, 128, 0)
 
 
 def tile_mix_ghost_res_kernel(tc, x, xt, g, gt, r, out):
@@ -46,8 +48,8 @@ def tile_mix_ghost_res_kernel(tc, x, xt, g, gt, r, out):
         codes = {}
         scales = {}
         for name, width in (("g", M), ("gt", N), ("x", M), ("xt", N)):
-            codes[name] = keep.tile([P, PASSES, width], U32, name=name + "_codes", align_bytes=64)
-            scales[name] = keep.tile([P, PASSES, width], U8, name=name + "_scales", align_bytes=64)
+            codes[name] = keep.tile([P, PASSES, width], U32, name=name + "_codes", align_bytes=MX_ALIGN)
+            scales[name] = keep.tile([P, PASSES, width], U8, name=name + "_scales", align_bytes=MX_ALIGN)
 
         def load(name, src, c, lo, width):
             tile = raw.tile([P, PACK, width], F32, name="raw_%s_%d_%d" % (name, c, lo), align_bytes=DMA_ALIGN)
@@ -57,7 +59,7 @@ def tile_mix_ghost_res_kernel(tc, x, xt, g, gt, r, out):
 
         def cast(src, vector_columns):
             width = src.shape[2]
-            tile = stage.tile([P, HALF, PACK], BF16, name="grouped", align_bytes=64)
+            tile = stage.tile([P, HALF, PACK], BF16, name="grouped", align_bytes=MX_ALIGN)
             for copy, lo, hi in ((nc.scalar.copy, vector_columns, width), (nc.vector.tensor_copy, 0, vector_columns)):
                 if hi > lo:
                     copy(
@@ -102,7 +104,7 @@ def tile_mix_ghost_res_kernel(tc, x, xt, g, gt, r, out):
         out_rows = out.rearrange("(m p) n -> p m n", p=P)
         for m, cols in ((0, slice(0, HALF)), (1, slice(0, N)), (0, slice(HALF, N))):
             nc.sync.dma_start(out=r_sb[:, m, cols], in_=r_rows[:, m, cols])
-        u_sb = keep.tile([P, M_TILES, N], F32, name="u_sb", align_bytes=64)
+        u_sb = keep.tile([P, M_TILES, N], F32, name="u_sb", align_bytes=MX_ALIGN)
         y_sb = keep.tile([P, M_TILES, N], F32, name="y_sb", align_bytes=DMA_ALIGN)
 
         u_acc = [[psum.tile([P, HALF], F32, name="bank%d" % (2 * m + h)) for h in range(2)] for m in range(M_TILES)]
@@ -168,8 +170,8 @@ def tile_mix_ghost_res_kernel(tc, x, xt, g, gt, r, out):
         product(0, 1)
         product(1, 2)
         product(0, 2)
-        finish(0, 1, 1, nc.vector)
         quantize_strip(LAST, 3, grouped)
+        finish(0, 1, 1, nc.vector)
         finish(1, 0, 2, nc.vector)
         finish(1, 2, 1, nc.vector)
         finish(0, 2, 1, nc.vector)

@@ -24,6 +24,7 @@ M_TILES = M // P
 HALF = N // 2
 
 DMA_ALIGN = 256
+ROW_GAP = DMA_ALIGN // 4
 MX_ALIGN = 64
 
 STRIP = 256
@@ -51,11 +52,11 @@ def tile_mix_ghost_res_kernel(tc, x, xt, g, gt, r, out):
             codes[name] = keep.tile([P, PASSES, width], U32, name=name + "_codes", align_bytes=MX_ALIGN)
             scales[name] = keep.tile([P, PASSES, width], U8, name=name + "_scales", align_bytes=MX_ALIGN)
 
-        def load(name, src, c, lo, width):
-            tile = raw.tile([P, PACK, width], F32, name="raw_%s_%d_%d" % (name, c, lo), align_bytes=DMA_ALIGN)
+        def load(name, src, c, lo, width, gap=0):
+            tile = raw.tile([P, PACK, width + gap], F32, name="raw_%s_%d_%d" % (name, c, lo), align_bytes=DMA_ALIGN)
             rows = src[c * K_PASS : (c + 1) * K_PASS, lo : lo + width]
-            nc.sync.dma_start(out=tile[:], in_=rows.rearrange("(p j) w -> p j w", j=PACK))
-            return tile
+            nc.sync.dma_start(out=tile[:, :, 0:width], in_=rows.rearrange("(p j) w -> p j w", j=PACK))
+            return tile[:, :, 0:width]
 
         def cast(src, vector_columns):
             width = src.shape[2]
@@ -96,9 +97,9 @@ def tile_mix_ghost_res_kernel(tc, x, xt, g, gt, r, out):
             x_raw.append(load("x", x, c, 0, M))
             xt_whole.append(load("xt", xt, c, 0, N))
         x_raw.append(load("x", x, LAST, 0, M))
-        xt_wide = load("xt", xt, LAST, 0, HALF)
+        xt_wide = load("xt", xt, LAST, 0, HALF, ROW_GAP)
         xt_last = [xt_wide[:, :, 0:STRIP], xt_wide[:, :, STRIP:HALF]]
-        xt_last += [load("xt", xt, LAST, s * STRIP, STRIP)[:] for s in range(2, STRIPS)]
+        xt_last += [load("xt", xt, LAST, s * STRIP, STRIP, ROW_GAP) for s in range(2, STRIPS)]
         r_sb = keep.tile([P, M_TILES, N], F32, name="r_sb", align_bytes=DMA_ALIGN)
         r_rows = r.rearrange("(m p) n -> p m n", p=P)
         out_rows = out.rearrange("(m p) n -> p m n", p=P)
@@ -163,8 +164,8 @@ def tile_mix_ghost_res_kernel(tc, x, xt, g, gt, r, out):
         grouped = cast(xt_last[2], VECTOR_OF_LAST[2])
         product(1, 0)
         quantize_strip(LAST, 2, grouped)
-        product(1, 1)
         product(0, 0)
+        product(1, 1)
         grouped = cast(xt_last[3], VECTOR_OF_LAST[3])
         finish(0, 0, 1, nc.gpsimd)
         product(0, 1)

@@ -1,6 +1,7 @@
 from contextlib import ExitStack
 
 import concourse.mybir as mybir
+from concourse.masks import make_identity
 
 K, M, N = 1536, 256, 1024
 FLOPS = 2 * (2 * K * M * N)
@@ -34,6 +35,17 @@ VECTOR_OF_HALF = 320
 VECTOR_OF_STRIP = 160
 VECTOR_OF_NARROW = M // 2
 VECTOR_OF_LAST = (160, 144, 128, 0)
+
+PARTS = [
+    [(True, (0, P), (0, M), 0)],
+    [(True, (P, 2 * P), (0, M), 0)],
+    [(True, (2 * P, 3 * P), (P, M), 0), (True, (3 * P, 4 * P), (P, M), P)],
+    [(False, (0, P), (STRIP, 2 * STRIP), 0)],
+    [(True, (4 * P, 5 * P), (P, M), 0), (True, (5 * P, 6 * P), (P, M), P)],
+    [(False, (0, P), (2 * STRIP, 3 * STRIP), 0)],
+    [(False, (P, M), (3 * STRIP, N), 0)],
+    [(False, (0, P), (3 * STRIP, N), 0)],
+]
 
 
 def tile_mix_ghost_res_kernel(tc, x, xt, g, gt, r, out):
@@ -76,18 +88,24 @@ def tile_mix_ghost_res_kernel(tc, x, xt, g, gt, r, out):
                 in_=grouped[:, 0:width, :].rearrange("p w j -> p (w j)"),
             )
 
-        def multiply(acc, stationary, moving, c, m, lo, width):
-            rows = slice(m * P, (m + 1) * P)
-            cols = slice(lo, lo + width)
+        def matmul(acc, stationary, rows, moving, cols, c, start, stop):
             nc.tensor.matmul_mx(
-                out=acc[:, 0:width],
+                out=acc,
                 lhsT=codes[stationary][:, c, rows].bitcast(formats[stationary]),
                 lhsT_scale=scales[stationary][:, c, rows],
                 rhs=codes[moving][:, c, cols].bitcast(formats[moving]),
                 rhs_scale=scales[moving][:, c, cols],
-                start=(c == 0),
-                stop=(c == LAST),
+                start=start,
+                stop=stop,
             )
+
+        def multiply(bank, parts, narrow, wide, c):
+            steps = [(n * STRIP + at, flipped, fixed, moved) for n, part in enumerate(parts) for flipped, fixed, moved, at in PARTS[part]]
+            for n, (at, flipped, fixed, moved) in enumerate(steps):
+                stationary, moving = (wide, narrow) if flipped else (narrow, wide)
+                first = c == 0 and n == 0
+                final = c == LAST and n == len(steps) - 1
+                matmul(bank[:, at : at + moved[1] - moved[0]], stationary, slice(*fixed), moving, slice(*moved), c, first, final)
 
         g_raw, gt_raw, x_raw, xt_whole = [], [], [], []
         for c in range(PASSES):
@@ -105,41 +123,50 @@ def tile_mix_ghost_res_kernel(tc, x, xt, g, gt, r, out):
         out_rows = out.rearrange("(m p) n -> p m n", p=P)
         for m, cols in ((0, slice(0, HALF)), (1, slice(0, N)), (0, slice(HALF, N))):
             nc.sync.dma_start(out=r_sb[:, m, cols], in_=r_rows[:, m, cols])
-        u_sb = keep.tile([P, M_TILES, N], F32, name="u_sb", align_bytes=MX_ALIGN)
+        u_sb = keep.tile([P, len(PARTS), STRIP], F32, name="u_sb", align_bytes=MX_ALIGN)
+        flipped_y = keep.tile([P, 4, STRIP], F32, name="flipped_y", align_bytes=MX_ALIGN)
         y_sb = keep.tile([P, M_TILES, N], F32, name="y_sb", align_bytes=DMA_ALIGN)
+        identity = keep.tile([P, P], F32, name="identity", align_bytes=MX_ALIGN)
+        make_identity(nc, identity[:])
 
-        u_acc = [[psum.tile([P, HALF], F32, name="bank%d" % (2 * m + h)) for h in range(2)] for m in range(M_TILES)]
+        u_parts = ((0, 1), (2, 3), (4, 5), (6, 7))
+        u_slot = {part: 2 * b + n for b, parts in enumerate(u_parts) for n, part in enumerate(parts)}
+        u_acc = [psum.tile([P, HALF], F32, name="bank%d" % b) for b in range(4)]
         for c in range(PASSES):
             quantize("g", c, 0, M, cast(g_raw[c][:], VECTOR_OF_NARROW))
             grouped = [cast(gt_raw[c][:, :, h * HALF : (h + 1) * HALF], VECTOR_OF_HALF) for h in range(2)]
             for h in range(2):
                 quantize("gt", c, h * HALF, HALF, grouped[h])
-                for m in range(M_TILES):
-                    multiply(u_acc[m][h], "g", "gt", c, m, h * HALF, HALF)
+                for b in (2 * h, 2 * h + 1):
+                    multiply(u_acc[b], u_parts[b], "g", "gt", c)
 
         quantize("x", 0, 0, M, cast(x_raw[0][:], VECTOR_OF_NARROW))
 
-        for h in range(2):
-            for m in range(M_TILES):
-                nc.scalar.copy(out=u_sb[:, m, h * HALF : (h + 1) * HALF], in_=u_acc[m][h][:])
+        for b in range(4):
+            nc.scalar.copy(out=u_sb[:, 2 * b : 2 * b + 2, :].rearrange("p n w -> p (n w)"), in_=u_acc[b][:])
 
-        a_acc = [[psum.tile([P, HALF], F32, name="bank%d" % bank) for bank in banks] for banks in ((4, 5), (6, 7), (0, 2), (1, 3))]
+        a_acc = [psum.tile([P, HALF], F32, name="bank%d" % bank) for bank in (4, 5, 6, 7, 0, 1, 2, 3)]
 
         def multiply_strip(c, s):
-            for m in reversed(range(M_TILES)):
-                multiply(a_acc[s][m], "x", "xt", c, m, s * STRIP, STRIP)
+            for part in (2 * s, 2 * s + 1):
+                multiply(a_acc[part], (part,), "x", "xt", c)
 
         def quantize_strip(c, s, grouped_strip):
             quantize("xt", c, s * STRIP, STRIP, grouped_strip)
             multiply_strip(c, s)
 
-        def product(m, s):
-            cols = slice(s * STRIP, (s + 1) * STRIP)
-            nc.vector.tensor_tensor(out=y_sb[:, m, cols], in0=a_acc[s][m][:, 0:STRIP], in1=u_sb[:, m, cols], op=MULT)
+        def product(part, dst):
+            nc.vector.tensor_tensor(out=dst, in0=a_acc[part][:, 0:STRIP], in1=u_sb[:, u_slot[part], :], op=MULT)
 
-        def finish(m, first, count, engine):
+        def y_of(m, s):
+            return y_sb[:, m, s * STRIP : (s + 1) * STRIP]
+
+        def finish(m, first, count, engine, y):
             cols = slice(first * STRIP, (first + count) * STRIP)
-            engine.tensor_tensor(out=y_sb[:, m, cols], in0=y_sb[:, m, cols], in1=r_sb[:, m, cols], op=ADD)
+            engine.tensor_tensor(out=y_sb[:, m, cols], in0=y, in1=r_sb[:, m, cols], op=ADD)
+
+        def store(m, first, count):
+            cols = slice(first * STRIP, (first + count) * STRIP)
             nc.sync.dma_start(out=out_rows[:, m, cols], in_=y_sb[:, m, cols])
 
         grouped = [cast(xt_whole[0][:, :, h * HALF : (h + 1) * HALF], VECTOR_OF_HALF) for h in range(2)]
@@ -162,21 +189,36 @@ def tile_mix_ghost_res_kernel(tc, x, xt, g, gt, r, out):
         for s in range(2):
             quantize_strip(LAST, s, grouped[s])
         grouped = cast(xt_last[2], VECTOR_OF_LAST[2])
-        product(1, 0)
+        product(0, flipped_y[:, 0, :])
         quantize_strip(LAST, 2, grouped)
-        product(0, 0)
-        product(1, 1)
+        product(3, y_of(0, 1))
         grouped = cast(xt_last[3], VECTOR_OF_LAST[3])
-        finish(0, 0, 1, nc.gpsimd)
-        product(0, 1)
-        product(1, 2)
-        product(0, 2)
+        finish(0, 1, 1, nc.gpsimd, y_of(0, 1))
+        product(1, flipped_y[:, 1, :])
+        product(2, flipped_y[:, 2, :])
+        upright = [psum.tile([P, HALF], F32, name="bank%d" % bank) for bank in (4, 5)]
+        for m in range(M_TILES):
+            for t in range(2):
+                nc.tensor.transpose(upright[m][:, t * P : (t + 1) * P], flipped_y[:, t, m * P : (m + 1) * P], identity[:])
+        for t in range(2):
+            nc.tensor.transpose(upright[1][:, STRIP + t * P : STRIP + (t + 1) * P], flipped_y[:, 2, t * P : (t + 1) * P], identity[:])
+        product(4, flipped_y[:, 3, :])
+        upright.append(psum.tile([P, HALF], F32, name="bank0"))
+        for t in range(2):
+            nc.tensor.transpose(upright[2][:, t * P : (t + 1) * P], flipped_y[:, 3, t * P : (t + 1) * P], identity[:])
+        product(5, y_of(0, 2))
+        finish(0, 0, 1, nc.vector, upright[0][:, 0:STRIP])
+        store(0, 0, 2)
         quantize_strip(LAST, 3, grouped)
-        finish(0, 1, 1, nc.vector)
-        finish(1, 0, 2, nc.vector)
-        finish(1, 2, 1, nc.vector)
-        finish(0, 2, 1, nc.vector)
+        finish(0, 2, 1, nc.gpsimd, y_of(0, 2))
+        for s in range(2):
+            finish(1, s, 1, nc.vector, upright[1][:, s * STRIP : (s + 1) * STRIP])
+            store(1, s, 1)
+        finish(1, 2, 1, nc.vector, upright[2][:, 0:STRIP])
+        store(1, 2, 1)
+        store(0, 2, 1)
+        product(6, y_of(1, 3))
+        product(7, y_of(0, 3))
         for m in reversed(range(M_TILES)):
-            product(m, 3)
-        for m in reversed(range(M_TILES)):
-            finish(m, 3, 1, nc.vector)
+            finish(m, 3, 1, nc.vector, y_of(m, 3))
+            store(m, 3, 1)

@@ -36,16 +36,7 @@ VECTOR_OF_STRIP = 160
 VECTOR_OF_NARROW = M // 2
 VECTOR_OF_LAST = (160, 144, 128, 0)
 
-PARTS = [
-    [(True, (0, P), (0, M), 0)],
-    [(True, (P, 2 * P), (0, M), 0)],
-    [(True, (2 * P, 3 * P), (P, M), 0), (True, (3 * P, 4 * P), (P, M), P)],
-    [(False, (0, P), (STRIP, 2 * STRIP), 0)],
-    [(True, (4 * P, 5 * P), (P, M), 0), (True, (5 * P, 6 * P), (P, M), P)],
-    [(False, (0, P), (2 * STRIP, 3 * STRIP), 0)],
-    [(False, (P, M), (3 * STRIP, N), 0)],
-    [(False, (0, P), (3 * STRIP, N), 0)],
-]
+PARTS = [[(True, (t * P, (t + 1) * P), (0, M), 0)] for t in range(STRIP // P)] + [[(False, (m * P, (m + 1) * P), (s * STRIP, (s + 1) * STRIP), 0)] for s in range(1, STRIPS) for m in ((0, 1) if s == 1 else (1, 0))]
 
 
 def tile_mix_ghost_res_kernel(tc, x, xt, g, gt, r, out):
@@ -124,7 +115,7 @@ def tile_mix_ghost_res_kernel(tc, x, xt, g, gt, r, out):
         for m, cols in ((0, slice(0, HALF)), (1, slice(0, N)), (0, slice(HALF, N))):
             nc.sync.dma_start(out=r_sb[:, m, cols], in_=r_rows[:, m, cols])
         u_sb = keep.tile([P, len(PARTS), STRIP], F32, name="u_sb", align_bytes=MX_ALIGN)
-        flipped_y = keep.tile([P, 4, STRIP], F32, name="flipped_y", align_bytes=MX_ALIGN)
+        flipped_y = keep.tile([P, 2, STRIP], F32, name="flipped_y", align_bytes=MX_ALIGN)
         y_sb = keep.tile([P, M_TILES, N], F32, name="y_sb", align_bytes=DMA_ALIGN)
         identity = keep.tile([P, P], F32, name="identity", align_bytes=MX_ALIGN)
         make_identity(nc, identity[:])
@@ -142,10 +133,7 @@ def tile_mix_ghost_res_kernel(tc, x, xt, g, gt, r, out):
 
         quantize("x", 0, 0, M, cast(x_raw[0][:], VECTOR_OF_NARROW))
 
-        for b in range(4):
-            nc.scalar.copy(out=u_sb[:, 2 * b : 2 * b + 2, :].rearrange("p n w -> p (n w)"), in_=u_acc[b][:])
-
-        a_acc = [psum.tile([P, HALF], F32, name="bank%d" % bank) for bank in (4, 5, 6, 7, 0, 1, 2, 3)]
+        a_acc = [psum.tile([P, HALF], F32, name="bank%d" % bank) for bank in range(4, 8)]
 
         def multiply_strip(c, s):
             for part in (2 * s, 2 * s + 1):
@@ -172,10 +160,14 @@ def tile_mix_ghost_res_kernel(tc, x, xt, g, gt, r, out):
         grouped = [cast(xt_whole[0][:, :, h * HALF : (h + 1) * HALF], VECTOR_OF_HALF) for h in range(2)]
         for h in range(2):
             quantize("xt", 0, h * HALF, HALF, grouped[h])
+        for b in range(4):
+            nc.scalar.copy(out=u_sb[:, 2 * b : 2 * b + 2, :].rearrange("p n w -> p (n w)"), in_=u_acc[b][:])
+
+        a_acc += [psum.tile([P, HALF], F32, name="bank%d" % bank) for bank in range(4)]
         for s in range(STRIPS):
             multiply_strip(0, s)
 
-        quantize("x", 1, 0, M, cast(x_raw[1][:], VECTOR_OF_NARROW))
+        quantize("x", 1, 0, M, cast(x_raw[1][:], M))
         grouped = []
         for s in range(STRIPS):
             grouped.append(cast(xt_whole[1][:, :, s * STRIP : (s + 1) * STRIP], VECTOR_OF_STRIP))
@@ -191,31 +183,25 @@ def tile_mix_ghost_res_kernel(tc, x, xt, g, gt, r, out):
         grouped = cast(xt_last[2], VECTOR_OF_LAST[2])
         product(0, flipped_y[:, 0, :])
         quantize_strip(LAST, 2, grouped)
-        product(3, y_of(0, 1))
-        grouped = cast(xt_last[3], VECTOR_OF_LAST[3])
-        finish(0, 1, 1, nc.gpsimd, y_of(0, 1))
         product(1, flipped_y[:, 1, :])
-        product(2, flipped_y[:, 2, :])
         upright = [psum.tile([P, HALF], F32, name="bank%d" % bank) for bank in (4, 5)]
         for m in range(M_TILES):
             for t in range(2):
                 nc.tensor.transpose(upright[m][:, t * P : (t + 1) * P], flipped_y[:, t, m * P : (m + 1) * P], identity[:])
-        for t in range(2):
-            nc.tensor.transpose(upright[1][:, STRIP + t * P : STRIP + (t + 1) * P], flipped_y[:, 2, t * P : (t + 1) * P], identity[:])
-        product(4, flipped_y[:, 3, :])
-        upright.append(psum.tile([P, HALF], F32, name="bank0"))
-        for t in range(2):
-            nc.tensor.transpose(upright[2][:, t * P : (t + 1) * P], flipped_y[:, 3, t * P : (t + 1) * P], identity[:])
+        product(2, y_of(0, 1))
+        grouped = cast(xt_last[3], VECTOR_OF_LAST[3])
+        finish(0, 1, 1, nc.gpsimd, y_of(0, 1))
+        product(3, y_of(1, 1))
+        product(4, y_of(1, 2))
         product(5, y_of(0, 2))
         finish(0, 0, 1, nc.vector, upright[0][:, 0:STRIP])
         store(0, 0, 2)
         quantize_strip(LAST, 3, grouped)
+        finish(1, 1, 2, nc.vector, y_sb[:, 1, STRIP : 3 * STRIP])
+        store(1, 1, 2)
         finish(0, 2, 1, nc.gpsimd, y_of(0, 2))
-        for s in range(2):
-            finish(1, s, 1, nc.vector, upright[1][:, s * STRIP : (s + 1) * STRIP])
-            store(1, s, 1)
-        finish(1, 2, 1, nc.vector, upright[2][:, 0:STRIP])
-        store(1, 2, 1)
+        finish(1, 0, 1, nc.vector, upright[1][:, 0:STRIP])
+        store(1, 0, 1)
         store(0, 2, 1)
         product(6, y_of(1, 3))
         product(7, y_of(0, 3))

@@ -36,7 +36,11 @@ VECTOR_OF_STRIP = 160
 VECTOR_OF_NARROW = M // 2
 VECTOR_OF_LAST = (160, 144, 128, 0)
 
-PARTS = [[(True, (t * P, (t + 1) * P), (0, M), 0)] for t in range(STRIP // P)] + [[(False, (m * P, (m + 1) * P), (s * STRIP, (s + 1) * STRIP), 0)] for s in range(1, STRIPS) for m in ((0, 1) if s == 1 else (1, 0))]
+PARTS = [
+    [(True, (s * STRIP + n * P, s * STRIP + (n + 1) * P), (0, M), 0)] if s == 1 else [(False, (m * P, (m + 1) * P), (s * STRIP, (s + 1) * STRIP), 0)]
+    for s in range(STRIPS)
+    for n, m in enumerate((0, 1) if s < 2 else (1, 0))
+]
 
 
 def tile_mix_ghost_res_kernel(tc, x, xt, g, gt, r, out):
@@ -61,9 +65,10 @@ def tile_mix_ghost_res_kernel(tc, x, xt, g, gt, r, out):
             nc.sync.dma_start(out=tile[:, :, 0:width], in_=rows.rearrange("(p j) w -> p j w", j=PACK))
             return tile[:, :, 0:width]
 
-        def cast(src, vector_columns):
+        def cast(src, vector_columns, tile=None):
             width = src.shape[2]
-            tile = stage.tile([P, HALF, PACK], BF16, name="grouped", align_bytes=MX_ALIGN)
+            if tile is None:
+                tile = stage.tile([P, HALF, PACK], BF16, name="grouped", align_bytes=MX_ALIGN)
             for copy, lo, hi in ((nc.scalar.copy, vector_columns, width), (nc.vector.tensor_copy, 0, vector_columns)):
                 if hi > lo:
                     copy(
@@ -181,30 +186,32 @@ def tile_mix_ghost_res_kernel(tc, x, xt, g, gt, r, out):
         for s in range(2):
             quantize_strip(LAST, s, grouped[s])
         grouped = cast(xt_last[2], VECTOR_OF_LAST[2])
-        product(0, flipped_y[:, 0, :])
+        product(0, y_of(0, 0))
         quantize_strip(LAST, 2, grouped)
-        product(1, flipped_y[:, 1, :])
-        upright = [psum.tile([P, HALF], F32, name="bank%d" % bank) for bank in (4, 5)]
-        for m in range(M_TILES):
-            for t in range(2):
-                nc.tensor.transpose(upright[m][:, t * P : (t + 1) * P], flipped_y[:, t, m * P : (m + 1) * P], identity[:])
-        product(2, y_of(0, 1))
-        grouped = cast(xt_last[3], VECTOR_OF_LAST[3])
-        finish(0, 1, 1, nc.gpsimd, y_of(0, 1))
-        product(3, y_of(1, 1))
+        grouped = cast(xt_last[3], VECTOR_OF_LAST[3], keep.tile([P, STRIP, PACK], BF16, name="shared", align_bytes=DMA_ALIGN))
+        finish(0, 0, 1, nc.gpsimd, y_of(0, 0))
+        store(0, 0, 1)
+        for n in range(2):
+            product(2 + n, flipped_y[:, n, :])
+        upright = psum.tile([P, M_TILES, STRIP], F32, name="bank6")
+        for n in range(2):
+            for m in range(M_TILES):
+                nc.tensor.transpose(upright[:, m, n * P : (n + 1) * P], flipped_y[:, n, m * P : (m + 1) * P], identity[:])
+        product(1, y_of(1, 0))
         product(4, y_of(1, 2))
-        product(5, y_of(0, 2))
-        finish(0, 0, 1, nc.vector, upright[0][:, 0:STRIP])
-        store(0, 0, 2)
         quantize_strip(LAST, 3, grouped)
-        finish(1, 1, 2, nc.vector, y_sb[:, 1, STRIP : 3 * STRIP])
-        store(1, 1, 2)
-        finish(0, 2, 1, nc.gpsimd, y_of(0, 2))
-        finish(1, 0, 1, nc.vector, upright[1][:, 0:STRIP])
-        store(1, 0, 1)
-        store(0, 2, 1)
+        late = keep.tile([P, 2, STRIP], F32, name="shared", align_bytes=DMA_ALIGN)
+        even = lambda rows: rows[:, 1, :].rearrange("p (h s w) -> p h s w", h=2, s=2)[:, :, 0, :]
+        nc.gpsimd.tensor_tensor(out=late[:], in0=even(y_sb), in1=even(r_sb), op=ADD)
+        product(5, y_of(0, 2))
+        for m in range(M_TILES):
+            finish(m, 1, 1, nc.vector, upright[:, m, :])
+            store(m, 1, 1)
+        nc.sync.dma_start(out=even(out_rows), in_=late[:])
         product(6, y_of(1, 3))
         product(7, y_of(0, 3))
+        finish(0, 2, 1, nc.vector, y_of(0, 2))
+        store(0, 2, 1)
         for m in reversed(range(M_TILES)):
             finish(m, 3, 1, nc.vector, y_of(m, 3))
             store(m, 3, 1)

from contextlib import ExitStack

import concourse.mybir as mybir
from concourse.masks import make_identity

K, M, N = 1536, 256, 1024
FLOPS = 2 * (2 * K * M * N)

F32 = mybir.dt.float32
BF16 = mybir.dt.bfloat16
U32 = mybir.dt.uint32
U8 = mybir.dt.uint8
E4M3X4 = mybir.dt.float8_e4m3fn_x4
E5M2X4 = mybir.dt.float8_e5m2_x4
MULT = mybir.AluOpType.mult
ADD = mybir.AluOpType.add

P = 128
PACK = 4
K_PASS = P * PACK
PASSES = K // K_PASS
LAST = PASSES - 1
CAST_RUN = 4
M_TILES = M // P
HALF = N // 2

DMA_ALIGN = 256
ROW_GAP = DMA_ALIGN // 4
MX_ALIGN = 64

STRIP = 256
STRIPS = N // STRIP

VECTOR_OF_HALF = 320
VECTOR_OF_STRIP = 160
VECTOR_OF_NARROW = M // 2
VECTOR_OF_LAST = (160, 144, 128, 0)

PARTS = [
    [(True, (s * STRIP + n * P, s * STRIP + (n + 1) * P), (0, M), 0)] if s == 1 else [(False, (m * P, (m + 1) * P), (s * STRIP, (s + 1) * STRIP), 0)]
    for s in range(STRIPS)
    for n, m in enumerate((0, 1) if s < 2 else (1, 0))
]


def tile_mix_ghost_res_kernel(tc, x, xt, g, gt, r, out):
    nc = tc.nc
    with ExitStack() as ctx:
        raw = ctx.enter_context(tc.tile_pool(name="raw", bufs=1))
        keep = ctx.enter_context(tc.tile_pool(name="keep", bufs=1))
        stage = ctx.enter_context(tc.tile_pool(name="stage", bufs=8))
        psum = ctx.enter_context(tc.psum_pool(name="psum", bufs=1))
        ctx.enter_context(tc.manual_schedule())

        formats = {"x": E4M3X4, "xt": E4M3X4, "g": E5M2X4, "gt": E5M2X4}
        codes = {}
        scales = {}
        for name, width in (("g", M), ("gt", N), ("x", M), ("xt", N)):
            codes[name] = keep.tile([P, PASSES, width], U32, name=name + "_codes", align_bytes=MX_ALIGN)
            scales[name] = keep.tile([P, PASSES, width], U8, name=name + "_scales", align_bytes=MX_ALIGN)

        def load(name, src, c, lo, width, gap=0):
            tile = raw.tile([P, PACK, width + gap], F32, name="raw_%s_%d_%d" % (name, c, lo), align_bytes=DMA_ALIGN)
            rows = src[c * K_PASS : (c + 1) * K_PASS, lo : lo + width]
            nc.sync.dma_start(out=tile[:, :, 0:width], in_=rows.rearrange("(p j) w -> p j w", j=PACK))
            return tile[:, :, 0:width]

        def cast(src, vector_columns, tile=None):
            width = src.shape[2]
            if tile is None:
                tile = stage.tile([P, HALF, PACK], BF16, name="grouped", align_bytes=MX_ALIGN)
            for copy, lo, hi in ((nc.scalar.copy, vector_columns, width), (nc.vector.tensor_copy, 0, vector_columns)):
                if hi > lo:
                    copy(
                        out=tile[:, lo:hi, :].rearrange("p (b i) j -> p b j i", i=CAST_RUN),
                        in_=src[:, :, lo:hi].rearrange("p j (b i) -> p b j i", i=CAST_RUN),
                    )
            return tile

        def quantize(name, c, lo, width, grouped):
            nc.vector.quantize_mx(
                out=codes[name][:, c, lo : lo + width].bitcast(formats[name]),
                scales=scales[name][:, c, lo : lo + width],
                in_=grouped[:, 0:width, :].rearrange("p w j -> p (w j)"),
            )

        def matmul(acc, stationary, rows, moving, cols, c, start, stop):
            nc.tensor.matmul_mx(
                out=acc,
                lhsT=codes[stationary][:, c, rows].bitcast(formats[stationary]),
                lhsT_scale=scales[stationary][:, c, rows],
                rhs=codes[moving][:, c, cols].bitcast(formats[moving]),
                rhs_scale=scales[moving][:, c, cols],
                start=start,
                stop=stop,
            )

        def multiply(bank, parts, narrow, wide, c):
            steps = [(n * STRIP + at, flipped, fixed, moved) for n, part in enumerate(parts) for flipped, fixed, moved, at in PARTS[part]]
            for n, (at, flipped, fixed, moved) in enumerate(steps):
                stationary, moving = (wide, narrow) if flipped else (narrow, wide)
                first = c == 0 and n == 0
                final = c == LAST and n == len(steps) - 1
                matmul(bank[:, at : at + moved[1] - moved[0]], stationary, slice(*fixed), moving, slice(*moved), c, first, final)

        g_raw, gt_raw, x_raw, xt_whole = [], [], [], []
        for c in range(PASSES):
            g_raw.append(load("g", g, c, 0, M))
            gt_raw.append(load("gt", gt, c, 0, N))
        for c in range(LAST):
            x_raw.append(load("x", x, c, 0, M))
            xt_whole.append(load("xt", xt, c, 0, N))
        x_raw.append(load("x", x, LAST, 0, M))
        xt_wide = load("xt", xt, LAST, 0, HALF, ROW_GAP)
        xt_last = [xt_wide[:, :, 0:STRIP], xt_wide[:, :, STRIP:HALF]]
        xt_last += [load("xt", xt, LAST, s * STRIP, STRIP, ROW_GAP) for s in range(2, STRIPS)]
        r_sb = keep.tile([P, M_TILES, N], F32, name="r_sb", align_bytes=DMA_ALIGN)
        r_rows = r.rearrange("(m p) n -> p m n", p=P)
        out_rows = out.rearrange("(m p) n -> p m n", p=P)
        for m, cols in ((0, slice(0, HALF)), (1, slice(0, N)), (0, slice(HALF, N))):
            nc.sync.dma_start(out=r_sb[:, m, cols], in_=r_rows[:, m, cols])
        u_sb = keep.tile([P, len(PARTS), STRIP], F32, name="u_sb", align_bytes=MX_ALIGN)
        flipped_y = keep.tile([P, 2, STRIP], F32, name="flipped_y", align_bytes=MX_ALIGN)
        y_sb = keep.tile([P, M_TILES, N], F32, name="y_sb", align_bytes=DMA_ALIGN)
        identity = keep.tile([P, P], F32, name="identity", align_bytes=MX_ALIGN)
        make_identity(nc, identity[:])

        u_parts = ((0, 1), (2, 3), (4, 5), (6, 7))
        u_slot = {part: 2 * b + n for b, parts in enumerate(u_parts) for n, part in enumerate(parts)}
        u_acc = [psum.tile([P, HALF], F32, name="bank%d" % b) for b in range(4)]
        for c in range(PASSES):
            quantize("g", c, 0, M, cast(g_raw[c][:], VECTOR_OF_NARROW))
            grouped = [cast(gt_raw[c][:, :, h * HALF : (h + 1) * HALF], VECTOR_OF_HALF) for h in range(2)]
            for h in range(2):
                quantize("gt", c, h * HALF, HALF, grouped[h])
                for b in (2 * h, 2 * h + 1):
                    multiply(u_acc[b], u_parts[b], "g", "gt", c)

        quantize("x", 0, 0, M, cast(x_raw[0][:], VECTOR_OF_NARROW))

        a_acc = [psum.tile([P, HALF], F32, name="bank%d" % bank) for bank in range(4, 8)]

        def multiply_strip(c, s):
            for part in (2 * s, 2 * s + 1):
                multiply(a_acc[part], (part,), "x", "xt", c)

        def quantize_strip(c, s, grouped_strip):
            quantize("xt", c, s * STRIP, STRIP, grouped_strip)
            multiply_strip(c, s)

        def product(part, dst):
            nc.vector.tensor_tensor(out=dst, in0=a_acc[part][:, 0:STRIP], in1=u_sb[:, u_slot[part], :], op=MULT)

        def y_of(m, s):
            return y_sb[:, m, s * STRIP : (s + 1) * STRIP]

        def finish(m, first, count, engine, y):
            cols = slice(first * STRIP, (first + count) * STRIP)
            engine.tensor_tensor(out=y_sb[:, m, cols], in0=y, in1=r_sb[:, m, cols], op=ADD)

        def store(m, first, count):
            cols = slice(first * STRIP, (first + count) * STRIP)
            nc.sync.dma_start(out=out_rows[:, m, cols], in_=y_sb[:, m, cols])

        grouped = [cast(xt_whole[0][:, :, h * HALF : (h + 1) * HALF], VECTOR_OF_HALF) for h in range(2)]
        for h in range(2):
            quantize("xt", 0, h * HALF, HALF, grouped[h])
        for b in range(4):
            nc.scalar.copy(out=u_sb[:, 2 * b : 2 * b + 2, :].rearrange("p n w -> p (n w)"), in_=u_acc[b][:])

        a_acc += [psum.tile([P, HALF], F32, name="bank%d" % bank) for bank in range(4)]
        for s in range(STRIPS):
            multiply_strip(0, s)

        quantize("x", 1, 0, M, cast(x_raw[1][:], M))
        grouped = []
        for s in range(STRIPS):
            grouped.append(cast(xt_whole[1][:, :, s * STRIP : (s + 1) * STRIP], VECTOR_OF_STRIP))
            if s > 0:
                quantize_strip(1, s - 1, grouped[s - 1])
        grouped_x = cast(x_raw[LAST][:], VECTOR_OF_NARROW)
        quantize_strip(1, STRIPS - 1, grouped[STRIPS - 1])
        quantize("x", LAST, 0, M, grouped_x)

        grouped = [cast(xt_last[s], VECTOR_OF_LAST[s]) for s in range(2)]
        for s in range(2):
            quantize_strip(LAST, s, grouped[s])
        grouped = cast(xt_last[2], VECTOR_OF_LAST[2])
        product(0, y_of(0, 0))
        quantize_strip(LAST, 2, grouped)
        grouped = cast(xt_last[3], VECTOR_OF_LAST[3], keep.tile([P, STRIP, PACK], BF16, name="shared", align_bytes=DMA_ALIGN))
        finish(0, 0, 1, nc.gpsimd, y_of(0, 0))
        store(0, 0, 1)
        for n in range(2):
            product(2 + n, flipped_y[:, n, :])
        upright = psum.tile([P, M_TILES, STRIP], F32, name="bank6")
        for n in range(2):
            for m in range(M_TILES):
                nc.tensor.transpose(upright[:, m, n * P : (n + 1) * P], flipped_y[:, n, m * P : (m + 1) * P], identity[:])
        product(1, y_of(1, 0))
        product(4, y_of(1, 2))
        quantize_strip(LAST, 3, grouped)
        late = keep.tile([P, 2, STRIP], F32, name="shared", align_bytes=DMA_ALIGN)
        even = lambda rows: rows[:, 1, :].rearrange("p (h s w) -> p h s w", h=2, s=2)[:, :, 0, :]
        nc.gpsimd.tensor_tensor(out=late[:], in0=even(y_sb), in1=even(r_sb), op=ADD)
        product(5, y_of(0, 2))
        for m in range(M_TILES):
            finish(m, 1, 1, nc.vector, upright[:, m, :])
            store(m, 1, 1)
        nc.sync.dma_start(out=even(out_rows), in_=late[:])
        product(6, y_of(1, 3))
        product(7, y_of(0, 3))
        finish(0, 2, 1, nc.vector, y_of(0, 2))
        store(0, 2, 1)
        for m in reversed(range(M_TILES)):
            finish(m, 3, 1, nc.vector, y_of(m, 3))
            store(m, 3, 1)
